import numpy as np
import ml_dtypes


def mxq(x, axis, fmt="e4m3"):
    dtype, down = {"e4m3": (ml_dtypes.float8_e4m3fn, 7), "e5m2": (ml_dtypes.float8_e5m2, 14)}[fmt]
    v = np.moveaxis(np.asarray(x, np.float32).astype(ml_dtypes.bfloat16).astype(np.float64), axis, -1)
    blocks = v.reshape(v.shape[:-1] + (-1, 32))
    amax = np.abs(blocks).max(-1, keepdims=True)
    byte = np.maximum(np.where(amax > 0, np.frexp(amax)[1] - 1 + 127, 0) - down, 1)
    scale = np.exp2(byte - 127.0)
    codes = (blocks / scale).astype(np.float32).astype(dtype).astype(np.float64)
    return np.moveaxis((codes * scale).reshape(v.shape), -1, axis)


WIDE = False


def mx_kscale(k):
    if not WIDE:
        return np.ones(k)
    levels = np.array([10, -10, 5, -5, 0])
    if k % 512:
        return np.exp2(np.random.permutation(np.resize(levels, k // 32))).repeat(32)
    a = np.empty((k // 512, 16))
    for p in range(k // 512):
        a[p, :8] = np.random.permutation(np.resize(levels, 8))
        for g in range(8):
            far = levels[np.abs(levels - a[p, g]) >= 10]
            a[p, g + 8] = far[np.random.randint(len(far))]
    return np.exp2(a.ravel()).repeat(32)


def f64(x):
    return np.asarray(x).astype(np.float64)


def striped(idx):
    return np.tile(idx.reshape(-1, 16).T, (8, 1)).astype(np.uint16)


def unstriped(offs):
    return offs[:16].T.reshape(-1).astype(np.int64)


def striped8(idx):
    return np.concatenate([x.reshape(-1, 16).T for x in idx]).astype(np.uint16)


def runs(offs, k):
    lists = np.stack([offs[16 * r : 16 * r + 16].T.reshape(-1) for r in range(8)]).astype(np.int64)
    return lists[np.arange(k) % 512 // 64]


def pack_weight(w):
    k, n = w.shape
    w = f64(np.asarray(w, np.float32).astype(ml_dtypes.bfloat16)).reshape(k // 32, 32, n)
    amax = np.abs(w).max(1)
    byte = np.clip(np.where(amax > 0, np.frexp(amax)[1] - 1 + 127 - 7, 1), 1, 254)
    scaled = (w * np.exp2(127.0 - byte)[:, None, :]).reshape(k, n).astype(np.float32)
    words = np.ascontiguousarray(scaled.reshape(k // 512, 128, 4, n).transpose(0, 1, 3, 2)).astype(ml_dtypes.float8_e4m3fn).view(np.uint8)
    return words, np.ascontiguousarray(byte.astype(np.uint8).reshape(k // 512, 16, n))


def unpack_weight(words, scales):
    g, p, n, _ = words.shape
    vals = np.ascontiguousarray(words).view(ml_dtypes.float8_e4m3fn).astype(np.float64) * np.repeat(np.exp2(scales.astype(np.float64) - 127.0), 8, axis=1)[..., None]
    return vals.transpose(0, 1, 3, 2).reshape(g * 512, n)


def sigmoid(v):
    return 1.0 / (1.0 + np.exp(-np.maximum(v, -700.0)))


K, T, S, N, H = 512, 2048, 512, 512, 512


def setup_inputs():
    n = np.random.standard_normal
    s = mx_kscale(K)[:, None]
    u = mx_kscale(S)
    packed_xT = pack_weight(n((K, T)) * s)
    return {
        "x_words": packed_xT[0],
        "x_scales": packed_xT[1],
        "wa": (n((K, H)) / np.sqrt(K) / s).astype(np.float32),
        "wb": (n((K, N)) / np.sqrt(K) / s).astype(np.float32),
        "gt": (np.random.uniform(0.5, 1.5, (S, 1)) * u[:, None]).astype(np.float32),
        "gi": (np.random.uniform(0.5, 1.5, (S, 1)) / u[:, None]).astype(np.float32),
        "offs": striped(np.random.permutation(T)[:S]),
        "two": striped(np.random.permutation(T)[:S]),
        "n1": striped8(np.stack([np.random.permutation(H) for _ in range(8)])),
        "n2": striped8(np.stack([np.random.permutation(H) for _ in range(8)])),
        "n3": striped8(np.stack([np.random.permutation(N) for _ in range(8)])),
        "n4": striped8(np.stack([np.random.permutation(N) for _ in range(8)])),
    }


def reference(x_words, x_scales, wa, wb, gt, gi, offs, two, n1, n2, n3, n4):
    xq = unpack_weight(x_words, x_scales)[:, unstriped(offs)]
    a = xq.T @ mxq(f64(wa), 0, "e4m3")
    z = f64(gt) * ((a - (a[np.arange(S)[:, None], runs(n1, S)])) * (sigmoid(a[np.arange(S)[:, None], runs(n2, S)])))
    x_two = unpack_weight(x_words, x_scales)[:, unstriped(two)]
    b = x_two.T @ mxq(f64(wb), 0, "e4m3")
    z2 = f64(gi) * b
    cv = 0.0625 * ((mxq(z, 0, "e4m3").T @ mxq(z2, 0, "e4m3")))
    st = np.maximum(cv, cv[np.arange(H)[:, None], runs(n3, H)])
    return st[np.arange(H)[:, None], runs(n4, H)] - (0.5 * cv)

@@ -1,0 +1,232 @@
+from contextlib import ExitStack
+
+import concourse.mybir as mybir
+
+K, T, S, N, H = 512, 2048, 512, 512, 512
+FLOPS = 2 * K * S * H + 2 * K * S * N + 2 * S * H * N
+
+F32 = mybir.dt.float32
+BF16 = mybir.dt.bfloat16
+I32 = mybir.dt.int32
+U32 = mybir.dt.uint32
+U16 = mybir.dt.uint16
+U8 = mybir.dt.uint8
+FP8X4 = mybir.dt.float8_e4m3fn_x4
+ACT = mybir.ActivationFunctionType
+ALU = mybir.AluOpType
+
+P = 128
+PACK = 4
+HALF = 256
+LIST_COLS = 32
+
+
+def tile_picked_momgdifhopb_none_p_kernel(
+    tc, x_words, x_scales, wa, wb, gt, gi, offs, two, n1, n2, n3, n4, out
+):
+    nc = tc.nc
+    with ExitStack() as ctx:
+        keep = ctx.enter_context(tc.tile_pool(name="keep", bufs=1))
+        psum = ctx.enter_context(tc.psum_pool(name="psum", bufs=1))
+
+        def sb(name, shape, dtype):
+            return keep.tile(shape, dtype, name=name, align_bytes=64)
+
+        def load_list(name, src):
+            lst = keep.tile([P, LIST_COLS], U16, name=name)
+            nc.sync.dma_start(lst[:], src)
+            return lst
+
+        def half_list(lst, h):
+            return lst[:, h * (LIST_COLS // 2) : (h + 1) * (LIST_COLS // 2)]
+
+        def half(h):
+            return slice(h * HALF, (h + 1) * HALF)
+
+        scale_table = sb("scale_table", [P, T], U8)
+        nc.vector.memset(scale_table[:].bitcast(I32), 0)
+        offs_l = load_list("offs_l", offs)
+        two_l = load_list("two_l", two)
+        n1_l = load_list("n1_l", n1)
+        for q in range(4):
+            nc.sync.dma_start(
+                scale_table[32 * q : 32 * q + 4, :].bitcast(I32), x_scales[0, 4 * q : 4 * q + 4, :].bitcast(I32)
+            )
+        wa_raw = sb("wa_raw", [P, PACK, H], F32)
+        nc.sync.dma_start(wa_raw[:], wa.rearrange("(p j) n -> p j n", j=PACK))
+        word_table = sb("word_table", [P, T], I32)
+        nc.sync.dma_start(word_table[:], x_words[0].rearrange("p c r -> p (c r)").bitcast(I32))
+        n2_l = load_list("n2_l", n2)
+        gt_sb = sb("gt_sb", [P, PACK], F32)
+        nc.sync.dma_start(gt_sb[:], gt.rearrange("(p t) o -> p (t o)", t=PACK))
+        wb_raw = sb("wb_raw", [P, PACK, N], F32)
+        nc.sync.dma_start(wb_raw[:], wb.rearrange("(p j) n -> p j n", j=PACK))
+        n3_l = load_list("n3_l", n3)
+        n4_l = load_list("n4_l", n4)
+        gi_sb = sb("gi_sb", [P, PACK], F32)
+        nc.sync.dma_start(gi_sb[:], gi.rearrange("(p t) o -> p (t o)", t=PACK))
+
+        warm_in = sb("warm_in", [P, 1], F32)
+        warm_out = sb("warm_out", [P, 1], F32)
+        nc.gpsimd.memset(warm_in[:], 0.0)
+        nc.scalar.activation(warm_out[:], warm_in[:], ACT.Sigmoid)
+
+        def gather_scales(name, lst):
+            picked = sb(name + "_picked", [P, S], U8)
+            nc.vector.tensor_copy(picked[:], scale_table[:].indirect(lst[:]))
+            return picked
+
+        def deal_scales(name, picked):
+            dealt = sb(name + "_dealt", [P, PACK, P], U8)
+            nc.vector.tensor_copy(dealt[:], picked[:].rearrange("p (m t) -> p t m", t=PACK))
+            return dealt
+
+        def gather_words(name, lst):
+            dealt = sb(name, [P, PACK, P], U32)
+            nc.vector.tensor_copy(dealt[:].rearrange("p t m -> p m t"), word_table[:].bitcast(U32).indirect(lst[:]))
+            return dealt
+
+        def interleave(copy, name, raw, cols):
+            width = cols.stop - cols.start
+            grouped = sb(name, [P, width, PACK], BF16)
+            copy(
+                grouped[:].rearrange("p (c i) j -> p c j i", i=4),
+                raw[:, :, cols].rearrange("p j (c i) -> p c j i", i=4),
+            )
+            return grouped
+
+        def quantize(codes, scales, grouped):
+            nc.vector.quantize_mx(out=codes.bitcast(FP8X4), scales=scales, in_=grouped.rearrange("p c j -> p (c j)"))
+
+        offs_picked = gather_scales("offs_scales", offs_l)
+        two_picked = gather_scales("two_scales", two_l)
+        offs_scales = deal_scales("offs_scales", offs_picked)
+        two_scales = deal_scales("two_scales", two_picked)
+
+        wa_codes = sb("wa_codes", [P, H], U32)
+        wa_scales = sb("wa_scales", [P, H], U8)
+        wa_grouped = [
+            interleave(nc.scalar.copy, "wa_grouped0", wa_raw, half(0)),
+            interleave(nc.vector.tensor_copy, "wa_grouped1", wa_raw, half(1)),
+        ]
+        for h in range(2):
+            quantize(wa_codes[:, half(h)], wa_scales[:, half(h)], wa_grouped[h][:])
+
+        offs_words = gather_words("offs_words", offs_l)
+        a_banks = [psum.tile([P, H], F32, name=f"a_bank{t}", tag=f"bank{t}") for t in range(PACK)]
+        for t in range(PACK):
+            nc.tensor.matmul_mx(
+                out=a_banks[t][:],
+                lhsT=offs_words[:, t, :].bitcast(FP8X4),
+                lhsT_scale=offs_scales[:, t, :],
+                rhs=wa_codes[:].bitcast(FP8X4),
+                rhs_scale=wa_scales[:],
+                start=True,
+                stop=True,
+            )
+        two_words = gather_words("two_words", two_l)
+
+        wb_codes = sb("wb_codes", [P, N], U32)
+        wb_scales = sb("wb_scales", [P, N], U8)
+        wb_grouped = [
+            interleave(nc.vector.tensor_copy, f"wb_grouped{h}", wb_raw, half(h)) for h in range(2)
+        ]
+        for h in range(2):
+            quantize(wb_codes[:, half(h)], wb_scales[:, half(h)], wb_grouped[h][:])
+        b_banks = [psum.tile([P, PACK, P], F32, name=f"b_bank{c}", tag=f"bank{PACK + c}") for c in range(PACK)]
+        for c in range(PACK):
+            cols = slice(c * P, (c + 1) * P)
+            for t in range(PACK):
+                nc.tensor.matmul_mx(
+                    out=b_banks[c][:, t, :],
+                    lhsT=two_words[:, t, :].bitcast(FP8X4),
+                    lhsT_scale=two_scales[:, t, :],
+                    rhs=wb_codes[:, cols].bitcast(FP8X4),
+                    rhs_scale=wb_scales[:, cols],
+                    start=True,
+                    stop=True,
+                )
+
+        diff = [sb(f"diff{h}", [P, PACK, HALF], F32) for h in range(2)]
+        gate = [sb(f"gate{h}", [P, PACK, HALF], F32) for h in range(2)]
+        z2_grouped = sb("z2_grouped", [P, N, PACK], BF16)
+        for t in range(PACK):
+            ga_window = sb(f"ga_window{t}", [P, H], F32)
+            ga_plain = sb(f"ga_plain{t}", [P, H], F32)
+            nc.scalar.activation(ga_window[:], a_banks[t][:], ACT.Copy, scale=gt_sb[:, t : t + 1])
+            nc.scalar.activation(ga_plain[:], a_banks[t][:], ACT.Copy, scale=gt_sb[:, t : t + 1])
+            for h in range(2):
+                nc.vector.tensor_tensor(
+                    diff[h][:, t, :], ga_window[:].indirect(half_list(n1_l, h)), ga_plain[:, half(h)], ALU.subtract
+                )
+            nc.vector.tensor_tensor(
+                z2_grouped[:, t * P : (t + 1) * P, :],
+                b_banks[t][:].rearrange("p t n -> p n t"),
+                gi_sb[:].unsqueeze(1).to_broadcast([P, P, PACK]),
+                ALU.mult,
+            )
+        z2_codes = sb("z2_codes", [P, N], U32)
+        z2_scales = sb("z2_scales", [P, N], U8)
+        quantize(z2_codes[:], z2_scales[:], z2_grouped[:])
+
+        a_windows = [sb(f"a_window{t}", [P, H], F32) for t in range(PACK)]
+        for t in range(PACK):
+            nc.scalar.copy(a_windows[t][:], a_banks[t][:])
+        z_codes = sb("z_codes", [P, PACK, P], U32)
+        z_scales = sb("z_scales", [P, PACK, P], U8)
+        rows = P // 2
+        for h in range(2):
+            for t in range(PACK):
+                nc.scalar.activation(gate[h][:, t, :], a_windows[t][:].indirect(half_list(n2_l, h)), ACT.Sigmoid)
+            z_grouped = sb(f"z_grouped{h}", [P, PACK, rows, PACK], BF16)
+            nc.vector.tensor_tensor(
+                z_grouped[:].rearrange("p u m t -> p m t u"),
+                diff[h][:].rearrange("p t (m u) -> p m t u", u=PACK),
+                gate[h][:].rearrange("p t (m u) -> p m t u", u=PACK),
+                ALU.mult,
+            )
+            ms = slice(h * rows, (h + 1) * rows)
+            for u in range(PACK):
+                quantize(z_codes[:, u, ms], z_scales[:, u, ms], z_grouped[:, u, :, :])
+
+        cv_window = [sb(f"cv_window{u}", [P, N], F32) for u in range(PACK)]
+        cv_halved = [sb(f"cv_halved{u}", [P, N], F32) for u in range(PACK)]
+        fetched = [sb(f"fetched{u}", [P, N], F32) for u in range(PACK)]
+        st_window = [sb(f"st_window{u}", [P, N], F32) for u in range(PACK)]
+        out_rows = out.rearrange("(p u) n -> p u n", u=PACK)
+        for u in range(PACK):
+            cv_bank = psum.tile([P, N], F32, name=f"cv_bank{u}", tag=f"bank{u}")
+            nc.tensor.matmul_mx(
+                out=cv_bank[:],
+                lhsT=z_codes[:, u, :].bitcast(FP8X4),
+                lhsT_scale=z_scales[:, u, :],
+                rhs=z2_codes[:].bitcast(FP8X4),
+                rhs_scale=z2_scales[:],
+                start=True,
+                stop=True,
+            )
+            nc.scalar.activation(cv_window[u][:], cv_bank[:], ACT.Copy, scale=-0.0625)
+            nc.scalar.activation(cv_halved[u][:], cv_bank[:], ACT.Copy, scale=-0.03125)
+
+        def fetch(u):
+            for h in range(2):
+                nc.vector.tensor_copy(fetched[u][:, half(h)], cv_window[u][:].indirect(half_list(n3_l, h)))
+
+        def larger(u):
+            nc.vector.tensor_tensor(st_window[u][:], fetched[u][:], cv_window[u][:], ALU.max)
+
+        def finish(u):
+            for h in range(2):
+                result = sb(f"result{u}_{h}", [P, HALF], F32)
+                nc.vector.tensor_tensor(
+                    result[:], st_window[u][:].indirect(half_list(n4_l, h)), cv_halved[u][:, half(h)], ALU.subtract
+                )
+                nc.sync.dma_start(out_rows[:, u, half(h)], result[:])
+
+        for step in range(PACK + 2):
+            if step < PACK:
+                fetch(step)
+            if 0 <= step - 2 < PACK:
+                finish(step - 2)
+            if 0 <= step - 1 < PACK:
+                larger(step - 1)

@@ -47,7 +47,8 @@ def tile_picked_momgdifhopb_none_p_kernel(
         nc.vector.memset(scale_table[:].bitcast(I32), 0)
         offs_l = load_list("offs_l", offs)
         two_l = load_list("two_l", two)
-        n1_l = load_list("n1_l", n1)
+        gt_sb = sb("gt_sb", [P, PACK], F32)
+        nc.sync.dma_start(gt_sb[:], gt.rearrange("(p t) o -> p (t o)", t=PACK))
         for q in range(4):
             nc.sync.dma_start(
                 scale_table[32 * q : 32 * q + 4, :].bitcast(I32), x_scales[0, 4 * q : 4 * q + 4, :].bitcast(I32)
@@ -56,20 +57,23 @@ def tile_picked_momgdifhopb_none_p_kernel(
         nc.sync.dma_start(wa_raw[:], wa.rearrange("(p j) n -> p j n", j=PACK))
         word_table = sb("word_table", [P, T], I32)
         nc.sync.dma_start(word_table[:], x_words[0].rearrange("p c r -> p (c r)").bitcast(I32))
-        n2_l = load_list("n2_l", n2)
-        gt_sb = sb("gt_sb", [P, PACK], F32)
-        nc.sync.dma_start(gt_sb[:], gt.rearrange("(p t) o -> p (t o)", t=PACK))
         wb_raw = sb("wb_raw", [P, PACK, N], F32)
         nc.sync.dma_start(wb_raw[:], wb.rearrange("(p j) n -> p j n", j=PACK))
-        n3_l = load_list("n3_l", n3)
-        n4_l = load_list("n4_l", n4)
+        n1_l = load_list("n1_l", n1)
         gi_sb = sb("gi_sb", [P, PACK], F32)
         nc.sync.dma_start(gi_sb[:], gi.rearrange("(p t) o -> p (t o)", t=PACK))
+        n2_l = load_list("n2_l", n2)
+        n3_l = load_list("n3_l", n3)
+        n4_l = load_list("n4_l", n4)
 
         warm_in = sb("warm_in", [P, 1], F32)
         warm_out = sb("warm_out", [P, 1], F32)
         nc.gpsimd.memset(warm_in[:], 0.0)
         nc.scalar.activation(warm_out[:], warm_in[:], ACT.Sigmoid)
+
+        windows = [sb(f"window{t}", [P, 2 * H], F32) for t in range(PACK)]
+        for t in range(PACK):
+            nc.vector.memset(windows[t][:, H:], 0.0)
 
         def gather_scales(name, lst):
             picked = sb(name + "_picked", [P, S], U8)
@@ -86,14 +90,8 @@ def tile_picked_momgdifhopb_none_p_kernel(
             nc.vector.tensor_copy(dealt[:].rearrange("p t m -> p m t"), word_table[:].bitcast(U32).indirect(lst[:]))
             return dealt
 
-        def interleave(copy, name, raw, cols):
-            width = cols.stop - cols.start
-            grouped = sb(name, [P, width, PACK], BF16)
-            copy(
-                grouped[:].rearrange("p (c i) j -> p c j i", i=4),
-                raw[:, :, cols].rearrange("p j (c i) -> p c j i", i=4),
-            )
-            return grouped
+        def interleave(copy, grouped, raw):
+            copy(grouped.rearrange("p (c i) j -> p c j i", i=4), raw.rearrange("p j (c i) -> p c j i", i=4))
 
         def quantize(codes, scales, grouped):
             nc.vector.quantize_mx(out=codes.bitcast(FP8X4), scales=scales, in_=grouped.rearrange("p c j -> p (c j)"))
@@ -105,10 +103,9 @@ def tile_picked_momgdifhopb_none_p_kernel(
 
         wa_codes = sb("wa_codes", [P, H], U32)
         wa_scales = sb("wa_scales", [P, H], U8)
-        wa_grouped = [
-            interleave(nc.scalar.copy, "wa_grouped0", wa_raw, half(0)),
-            interleave(nc.vector.tensor_copy, "wa_grouped1", wa_raw, half(1)),
-        ]
+        wa_grouped = [sb(f"wa_grouped{h}", [P, HALF, PACK], BF16) for h in range(2)]
+        interleave(nc.scalar.copy, wa_grouped[0][:], wa_raw[:, :, half(0)])
+        interleave(nc.vector.tensor_copy, wa_grouped[1][:], wa_raw[:, :, half(1)])
         for h in range(2):
             quantize(wa_codes[:, half(h)], wa_scales[:, half(h)], wa_grouped[h][:])
 
@@ -126,48 +123,52 @@ def tile_picked_momgdifhopb_none_p_kernel(
             )
         two_words = gather_words("two_words", two_l)
 
+        ga_plain = [sb(f"ga_plain{t}", [P, H], F32) for t in range(PACK)]
+        for t in range(PACK):
+            nc.scalar.activation(windows[t][:, :H], a_banks[t][:], ACT.Copy, scale=gt_sb[:, t : t + 1])
+            if t == 0:
+                nc.scalar.activation(ga_plain[t][:], a_banks[t][:], ACT.Copy, scale=gt_sb[:, t : t + 1])
+            else:
+                nc.sync.dma_start(ga_plain[t][:], windows[t][:, :H])
+
         wb_codes = sb("wb_codes", [P, N], U32)
         wb_scales = sb("wb_scales", [P, N], U8)
-        wb_grouped = [
-            interleave(nc.vector.tensor_copy, f"wb_grouped{h}", wb_raw, half(h)) for h in range(2)
-        ]
+        wb_grouped = [sb(f"wb_grouped{h}", [P, HALF, PACK], BF16) for h in range(2)]
         for h in range(2):
-            quantize(wb_codes[:, half(h)], wb_scales[:, half(h)], wb_grouped[h][:])
-        b_banks = [psum.tile([P, PACK, P], F32, name=f"b_bank{c}", tag=f"bank{PACK + c}") for c in range(PACK)]
-        for c in range(PACK):
-            cols = slice(c * P, (c + 1) * P)
-            for t in range(PACK):
-                nc.tensor.matmul_mx(
-                    out=b_banks[c][:, t, :],
-                    lhsT=two_words[:, t, :].bitcast(FP8X4),
-                    lhsT_scale=two_scales[:, t, :],
-                    rhs=wb_codes[:, cols].bitcast(FP8X4),
-                    rhs_scale=wb_scales[:, cols],
-                    start=True,
-                    stop=True,
-                )
-
-        diff = [sb(f"diff{h}", [P, PACK, HALF], F32) for h in range(2)]
-        gate = [sb(f"gate{h}", [P, PACK, HALF], F32) for h in range(2)]
+            interleave(nc.vector.tensor_copy, wb_grouped[h][:], wb_raw[:, :, half(h)])
         z2_grouped = sb("z2_grouped", [P, N, PACK], BF16)
-        for t in range(PACK):
-            ga_window = sb(f"ga_window{t}", [P, H], F32)
-            ga_plain = sb(f"ga_plain{t}", [P, H], F32)
-            nc.scalar.activation(ga_window[:], a_banks[t][:], ACT.Copy, scale=gt_sb[:, t : t + 1])
-            nc.scalar.activation(ga_plain[:], a_banks[t][:], ACT.Copy, scale=gt_sb[:, t : t + 1])
-            for h in range(2):
-                nc.vector.tensor_tensor(
-                    diff[h][:, t, :], ga_window[:].indirect(half_list(n1_l, h)), ga_plain[:, half(h)], ALU.subtract
-                )
-            nc.vector.tensor_tensor(
-                z2_grouped[:, t * P : (t + 1) * P, :],
-                b_banks[t][:].rearrange("p t n -> p n t"),
-                gi_sb[:].unsqueeze(1).to_broadcast([P, P, PACK]),
-                ALU.mult,
-            )
         z2_codes = sb("z2_codes", [P, N], U32)
         z2_scales = sb("z2_scales", [P, N], U8)
+        diff = sb("diff", [P, PACK, H], F32)
+
+        def difference(t):
+            nc.vector.tensor_tensor(diff[:, t, :], windows[t][:].indirect(n1_l[:]), ga_plain[t][:], ALU.subtract)
+
+        for h in range(2):
+            quantize(wb_codes[:, half(h)], wb_scales[:, half(h)], wb_grouped[h][:])
+            difference(h)
+            for c in range(2 * h, 2 * h + 2):
+                cols = slice(c * P, (c + 1) * P)
+                b_bank = psum.tile([P, PACK, P], F32, name=f"b_bank{c}", tag=f"bank{PACK + c}")
+                for t in range(PACK):
+                    nc.tensor.matmul_mx(
+                        out=b_bank[:, t, :],
+                        lhsT=two_words[:, t, :].bitcast(FP8X4),
+                        lhsT_scale=two_scales[:, t, :],
+                        rhs=wb_codes[:, cols].bitcast(FP8X4),
+                        rhs_scale=wb_scales[:, cols],
+                        start=True,
+                        stop=True,
+                    )
+                nc.vector.tensor_tensor(
+                    z2_grouped[:, cols, :],
+                    b_bank[:].rearrange("p t n -> p n t"),
+                    gi_sb[:].unsqueeze(1).to_broadcast([P, P, PACK]),
+                    ALU.mult,
+                )
+        difference(2)
         quantize(z2_codes[:], z2_scales[:], z2_grouped[:])
+        difference(3)
 
         a_windows = [sb(f"a_window{t}", [P, H], F32) for t in range(PACK)]
         for t in range(PACK):
@@ -175,57 +176,78 @@ def tile_picked_momgdifhopb_none_p_kernel(
         z_codes = sb("z_codes", [P, PACK, P], U32)
         z_scales = sb("z_scales", [P, PACK, P], U8)
         rows = P // 2
+        gate = [sb(f"gate{h}", [P, PACK, HALF], F32) for h in range(2)]
         for h in range(2):
             for t in range(PACK):
                 nc.scalar.activation(gate[h][:, t, :], a_windows[t][:].indirect(half_list(n2_l, h)), ACT.Sigmoid)
-            z_grouped = sb(f"z_grouped{h}", [P, PACK, rows, PACK], BF16)
+
+        def product(dst, h, us):
             nc.vector.tensor_tensor(
-                z_grouped[:].rearrange("p u m t -> p m t u"),
-                diff[h][:].rearrange("p t (m u) -> p m t u", u=PACK),
-                gate[h][:].rearrange("p t (m u) -> p m t u", u=PACK),
+                dst.rearrange("p u m t -> p m t u"),
+                diff[:, :, half(h)].rearrange("p t (m u) -> p m t u", u=PACK)[:, :, :, us],
+                gate[h][:].rearrange("p t (m u) -> p m t u", u=PACK)[:, :, :, us],
                 ALU.mult,
             )
-            ms = slice(h * rows, (h + 1) * rows)
-            for u in range(PACK):
-                quantize(z_codes[:, u, ms], z_scales[:, u, ms], z_grouped[:, u, :, :])
 
-        cv_window = [sb(f"cv_window{u}", [P, N], F32) for u in range(PACK)]
-        cv_halved = [sb(f"cv_halved{u}", [P, N], F32) for u in range(PACK)]
-        fetched = [sb(f"fetched{u}", [P, N], F32) for u in range(PACK)]
-        st_window = [sb(f"st_window{u}", [P, N], F32) for u in range(PACK)]
-        out_rows = out.rearrange("(p u) n -> p u n", u=PACK)
-        for u in range(PACK):
-            cv_bank = psum.tile([P, N], F32, name=f"cv_bank{u}", tag=f"bank{u}")
-            nc.tensor.matmul_mx(
-                out=cv_bank[:],
-                lhsT=z_codes[:, u, :].bitcast(FP8X4),
-                lhsT_scale=z_scales[:, u, :],
-                rhs=z2_codes[:].bitcast(FP8X4),
-                rhs_scale=z2_scales[:],
-                start=True,
-                stop=True,
+        for us in (slice(0, 2), slice(2, 4)):
+            z_grouped = sb("z_grouped", [P, 2, P, PACK], BF16)
+            for h in range(2):
+                product(z_grouped[:, :, h * rows : (h + 1) * rows, :], h, us)
+            quantize(
+                z_codes[:, us, :].rearrange("p u m -> p (u m)"),
+                z_scales[:, us, :].rearrange("p u m -> p (u m)"),
+                z_grouped[:].rearrange("p u m t -> p (u m) t"),
             )
-            nc.scalar.activation(cv_window[u][:], cv_bank[:], ACT.Copy, scale=-0.0625)
-            nc.scalar.activation(cv_halved[u][:], cv_bank[:], ACT.Copy, scale=-0.03125)
+
+        cv_halved = [sb(f"cv_halved{u}", [P, N], F32) for u in range(PACK)]
+        st_window = [sb(f"st_window{u}", [P, 2 * N], F32) for u in range(PACK)]
+        out_rows = out.rearrange("(p u) n -> p u n", u=PACK)
+        cv_banks = [
+            [psum.tile([P, HALF], F32, name=f"cv_bank{u}_{h}", tag=f"bank{2 * u + h}") for h in range(2)]
+            for u in range(PACK)
+        ]
+
+        def moments(u):
+            for h in range(2):
+                nc.tensor.matmul_mx(
+                    out=cv_banks[u][h][:],
+                    lhsT=z_codes[:, u, :].bitcast(FP8X4),
+                    lhsT_scale=z_scales[:, u, :],
+                    rhs=z2_codes[:, half(h)].bitcast(FP8X4),
+                    rhs_scale=z2_scales[:, half(h)],
+                    start=True,
+                    stop=True,
+                )
+                nc.scalar.activation(windows[u][:, half(h)], cv_banks[u][h][:], ACT.Copy, scale=-0.0625)
+
+        def halve(u):
+            for h in range(2):
+                nc.scalar.activation(cv_halved[u][:, half(h)], cv_banks[u][h][:], ACT.Copy, scale=-0.03125)
 
         def fetch(u):
-            for h in range(2):
-                nc.vector.tensor_copy(fetched[u][:, half(h)], cv_window[u][:].indirect(half_list(n3_l, h)))
+            nc.vector.tensor_copy(st_window[u][:, N:], windows[u][:].indirect(n3_l[:]))
 
         def larger(u):
-            nc.vector.tensor_tensor(st_window[u][:], fetched[u][:], cv_window[u][:], ALU.max)
+            nc.vector.tensor_tensor(st_window[u][:, :N], st_window[u][:, N:], windows[u][:, :N], ALU.max)
 
         def finish(u):
-            for h in range(2):
-                result = sb(f"result{u}_{h}", [P, HALF], F32)
+            pieces = 2 if u == PACK - 1 else 1
+            width = N // pieces
+            for i in range(pieces):
+                cols = slice(i * width, (i + 1) * width)
+                offsets = n4_l[:, i * width // 16 : (i + 1) * width // 16]
+                result = sb(f"result{u}_{i}", [P, width], F32)
                 nc.vector.tensor_tensor(
-                    result[:], st_window[u][:].indirect(half_list(n4_l, h)), cv_halved[u][:, half(h)], ALU.subtract
+                    result[:], st_window[u][:].indirect(offsets), cv_halved[u][:, cols], ALU.subtract
                 )
-                nc.sync.dma_start(out_rows[:, u, half(h)], result[:])
+                nc.sync.dma_start(out_rows[:, u, cols], result[:])
 
         for step in range(PACK + 2):
             if step < PACK:
+                moments(step)
                 fetch(step)
+            if 0 <= step - 1 < PACK:
+                halve(step - 1)
             if 0 <= step - 2 < PACK:
                 finish(step - 2)
             if 0 <= step - 1 < PACK:

from contextlib import ExitStack

import concourse.mybir as mybir

K, T, S, N, H = 512, 2048, 512, 512, 512
FLOPS = 2 * K * S * H + 2 * K * S * N + 2 * S * H * N

F32 = mybir.dt.float32
BF16 = mybir.dt.bfloat16
I32 = mybir.dt.int32
U32 = mybir.dt.uint32
U16 = mybir.dt.uint16
U8 = mybir.dt.uint8
FP8X4 = mybir.dt.float8_e4m3fn_x4
ACT = mybir.ActivationFunctionType
ALU = mybir.AluOpType

P = 128
PACK = 4
HALF = 256
LIST_COLS = 32


def tile_picked_momgdifhopb_none_p_kernel(
    tc, x_words, x_scales, wa, wb, gt, gi, offs, two, n1, n2, n3, n4, out
):
    nc = tc.nc
    with ExitStack() as ctx:
        keep = ctx.enter_context(tc.tile_pool(name="keep", bufs=1))
        psum = ctx.enter_context(tc.psum_pool(name="psum", bufs=1))

        def sb(name, shape, dtype):
            return keep.tile(shape, dtype, name=name, align_bytes=64)

        def load_list(name, src):
            lst = keep.tile([P, LIST_COLS], U16, name=name)
            nc.sync.dma_start(lst[:], src)
            return lst

        def half_list(lst, h):
            return lst[:, h * (LIST_COLS // 2) : (h + 1) * (LIST_COLS // 2)]

        def half(h):
            return slice(h * HALF, (h + 1) * HALF)

        scale_table = sb("scale_table", [P, T], U8)
        nc.vector.memset(scale_table[:].bitcast(I32), 0)
        offs_l = load_list("offs_l", offs)
        two_l = load_list("two_l", two)
        gt_sb = sb("gt_sb", [P, PACK], F32)
        nc.sync.dma_start(gt_sb[:], gt.rearrange("(p t) o -> p (t o)", t=PACK))
        for q in range(4):
            nc.sync.dma_start(
                scale_table[32 * q : 32 * q + 4, :].bitcast(I32), x_scales[0, 4 * q : 4 * q + 4, :].bitcast(I32)
            )
        wa_raw = sb("wa_raw", [P, PACK, H], F32)
        nc.sync.dma_start(wa_raw[:], wa.rearrange("(p j) n -> p j n", j=PACK))
        word_table = sb("word_table", [P, T], I32)
        nc.sync.dma_start(word_table[:], x_words[0].rearrange("p c r -> p (c r)").bitcast(I32))
        wb_raw = sb("wb_raw", [P, PACK, N], F32)
        nc.sync.dma_start(wb_raw[:], wb.rearrange("(p j) n -> p j n", j=PACK))
        n1_l = load_list("n1_l", n1)
        gi_sb = sb("gi_sb", [P, PACK], F32)
        nc.sync.dma_start(gi_sb[:], gi.rearrange("(p t) o -> p (t o)", t=PACK))
        n2_l = load_list("n2_l", n2)
        n3_l = load_list("n3_l", n3)
        n4_l = load_list("n4_l", n4)

        warm_in = sb("warm_in", [P, 1], F32)
        warm_out = sb("warm_out", [P, 1], F32)
        nc.gpsimd.memset(warm_in[:], 0.0)
        nc.scalar.activation(warm_out[:], warm_in[:], ACT.Sigmoid)

        windows = [sb(f"window{t}", [P, 2 * H], F32) for t in range(PACK)]
        for t in range(PACK):
            nc.vector.memset(windows[t][:, H:], 0.0)

        def gather_scales(name, lst):
            picked = sb(name + "_picked", [P, S], U8)
            nc.vector.tensor_copy(picked[:], scale_table[:].indirect(lst[:]))
            return picked

        def deal_scales(name, picked):
            dealt = sb(name + "_dealt", [P, PACK, P], U8)
            nc.vector.tensor_copy(dealt[:], picked[:].rearrange("p (m t) -> p t m", t=PACK))
            return dealt

        def gather_words(name, lst):
            dealt = sb(name, [P, PACK, P], U32)
            nc.vector.tensor_copy(dealt[:].rearrange("p t m -> p m t"), word_table[:].bitcast(U32).indirect(lst[:]))
            return dealt

        def interleave(copy, grouped, raw):
            copy(grouped.rearrange("p (c i) j -> p c j i", i=4), raw.rearrange("p j (c i) -> p c j i", i=4))

        def quantize(codes, scales, grouped):
            nc.vector.quantize_mx(out=codes.bitcast(FP8X4), scales=scales, in_=grouped.rearrange("p c j -> p (c j)"))

        offs_picked = gather_scales("offs_scales", offs_l)
        two_picked = gather_scales("two_scales", two_l)
        offs_scales = deal_scales("offs_scales", offs_picked)
        two_scales = deal_scales("two_scales", two_picked)

        wa_codes = sb("wa_codes", [P, H], U32)
        wa_scales = sb("wa_scales", [P, H], U8)
        wa_grouped = [sb(f"wa_grouped{h}", [P, HALF, PACK], BF16) for h in range(2)]
        interleave(nc.scalar.copy, wa_grouped[0][:], wa_raw[:, :, half(0)])
        interleave(nc.vector.tensor_copy, wa_grouped[1][:], wa_raw[:, :, half(1)])
        for h in range(2):
            quantize(wa_codes[:, half(h)], wa_scales[:, half(h)], wa_grouped[h][:])

        offs_words = gather_words("offs_words", offs_l)
        a_banks = [psum.tile([P, H], F32, name=f"a_bank{t}", tag=f"bank{t}") for t in range(PACK)]
        for t in range(PACK):
            nc.tensor.matmul_mx(
                out=a_banks[t][:],
                lhsT=offs_words[:, t, :].bitcast(FP8X4),
                lhsT_scale=offs_scales[:, t, :],
                rhs=wa_codes[:].bitcast(FP8X4),
                rhs_scale=wa_scales[:],
                start=True,
                stop=True,
            )
        two_words = gather_words("two_words", two_l)

        ga_plain = [sb(f"ga_plain{t}", [P, H], F32) for t in range(PACK)]
        for t in range(PACK):
            nc.scalar.activation(windows[t][:, :H], a_banks[t][:], ACT.Copy, scale=gt_sb[:, t : t + 1])
            if t == 0:
                nc.scalar.activation(ga_plain[t][:], a_banks[t][:], ACT.Copy, scale=gt_sb[:, t : t + 1])
            else:
                nc.sync.dma_start(ga_plain[t][:], windows[t][:, :H])

        wb_codes = sb("wb_codes", [P, N], U32)
        wb_scales = sb("wb_scales", [P, N], U8)
        wb_grouped = [sb(f"wb_grouped{h}", [P, HALF, PACK], BF16) for h in range(2)]
        for h in range(2):
            interleave(nc.vector.tensor_copy, wb_grouped[h][:], wb_raw[:, :, half(h)])
        z2_grouped = sb("z2_grouped", [P, N, PACK], BF16)
        z2_codes = sb("z2_codes", [P, N], U32)
        z2_scales = sb("z2_scales", [P, N], U8)
        diff = sb("diff", [P, PACK, H], F32)

        def difference(t):
            nc.vector.tensor_tensor(diff[:, t, :], windows[t][:].indirect(n1_l[:]), ga_plain[t][:], ALU.subtract)

        for h in range(2):
            quantize(wb_codes[:, half(h)], wb_scales[:, half(h)], wb_grouped[h][:])
            difference(h)
            for c in range(2 * h, 2 * h + 2):
                cols = slice(c * P, (c + 1) * P)
                b_bank = psum.tile([P, PACK, P], F32, name=f"b_bank{c}", tag=f"bank{PACK + c}")
                for t in range(PACK):
                    nc.tensor.matmul_mx(
                        out=b_bank[:, t, :],
                        lhsT=two_words[:, t, :].bitcast(FP8X4),
                        lhsT_scale=two_scales[:, t, :],
                        rhs=wb_codes[:, cols].bitcast(FP8X4),
                        rhs_scale=wb_scales[:, cols],
                        start=True,
                        stop=True,
                    )
                nc.vector.tensor_tensor(
                    z2_grouped[:, cols, :],
                    b_bank[:].rearrange("p t n -> p n t"),
                    gi_sb[:].unsqueeze(1).to_broadcast([P, P, PACK]),
                    ALU.mult,
                )
        difference(2)
        quantize(z2_codes[:], z2_scales[:], z2_grouped[:])
        difference(3)

        a_windows = [sb(f"a_window{t}", [P, H], F32) for t in range(PACK)]
        for t in range(PACK):
            nc.scalar.copy(a_windows[t][:], a_banks[t][:])
        z_codes = sb("z_codes", [P, PACK, P], U32)
        z_scales = sb("z_scales", [P, PACK, P], U8)
        rows = P // 2
        gate = [sb(f"gate{h}", [P, PACK, HALF], F32) for h in range(2)]
        for h in range(2):
            for t in range(PACK):
                nc.scalar.activation(gate[h][:, t, :], a_windows[t][:].indirect(half_list(n2_l, h)), ACT.Sigmoid)

        def product(dst, h, us):
            nc.vector.tensor_tensor(
                dst.rearrange("p u m t -> p m t u"),
                diff[:, :, half(h)].rearrange("p t (m u) -> p m t u", u=PACK)[:, :, :, us],
                gate[h][:].rearrange("p t (m u) -> p m t u", u=PACK)[:, :, :, us],
                ALU.mult,
            )

        for us in (slice(0, 2), slice(2, 4)):
            z_grouped = sb("z_grouped", [P, 2, P, PACK], BF16)
            for h in range(2):
                product(z_grouped[:, :, h * rows : (h + 1) * rows, :], h, us)
            quantize(
                z_codes[:, us, :].rearrange("p u m -> p (u m)"),
                z_scales[:, us, :].rearrange("p u m -> p (u m)"),
                z_grouped[:].rearrange("p u m t -> p (u m) t"),
            )

        cv_halved = [sb(f"cv_halved{u}", [P, N], F32) for u in range(PACK)]
        st_window = [sb(f"st_window{u}", [P, 2 * N], F32) for u in range(PACK)]
        out_rows = out.rearrange("(p u) n -> p u n", u=PACK)
        cv_banks = [
            [psum.tile([P, HALF], F32, name=f"cv_bank{u}_{h}", tag=f"bank{2 * u + h}") for h in range(2)]
            for u in range(PACK)
        ]

        def moments(u):
            for h in range(2):
                nc.tensor.matmul_mx(
                    out=cv_banks[u][h][:],
                    lhsT=z_codes[:, u, :].bitcast(FP8X4),
                    lhsT_scale=z_scales[:, u, :],
                    rhs=z2_codes[:, half(h)].bitcast(FP8X4),
                    rhs_scale=z2_scales[:, half(h)],
                    start=True,
                    stop=True,
                )
                nc.scalar.activation(windows[u][:, half(h)], cv_banks[u][h][:], ACT.Copy, scale=-0.0625)

        def halve(u):
            for h in range(2):
                nc.scalar.activation(cv_halved[u][:, half(h)], cv_banks[u][h][:], ACT.Copy, scale=-0.03125)

        def fetch(u):
            nc.vector.tensor_copy(st_window[u][:, N:], windows[u][:].indirect(n3_l[:]))

        def larger(u):
            nc.vector.tensor_tensor(st_window[u][:, :N], st_window[u][:, N:], windows[u][:, :N], ALU.max)

        def finish(u):
            pieces = 2 if u == PACK - 1 else 1
            width = N // pieces
            for i in range(pieces):
                cols = slice(i * width, (i + 1) * width)
                offsets = n4_l[:, i * width // 16 : (i + 1) * width // 16]
                result = sb(f"result{u}_{i}", [P, width], F32)
                nc.vector.tensor_tensor(
                    result[:], st_window[u][:].indirect(offsets), cv_halved[u][:, cols], ALU.subtract
                )
                nc.sync.dma_start(out_rows[:, u, cols], result[:])

        for step in range(PACK + 2):
            if step < PACK:
                moments(step)
                fetch(step)
            if 0 <= step - 1 < PACK:
                halve(step - 1)
            if 0 <= step - 2 < PACK:
                finish(step - 2)
            if 0 <= step - 1 < PACK:
                larger(step - 1)
